import numpy as np
CORES = [50,51,178,179,306,307,434,435]
N = 8
def setup_inputs(rng):
    return {"x": rng.standard_normal((N, 128, 512), dtype=np.float32)}
def reference(x):
    s = x.sum(axis=0, dtype=np.float64).astype(x.dtype)
    b = 512 // N
    return {"y": np.stack([s[:, r * b:(r + 1) * b] for r in range(N)])}

@@ -1,0 +1,71 @@
+from concourse.bass import DstId, RemoteDMATransfer
+
+SCRATCH = {
+    "xh": ("dram", [4, 128, 128], "float32"),
+    "lp": ("dram", [128, 128], "float32"),
+    "ld": ("dram", [128, 128], "float32"),
+    "fin": ("dram", [128, 128], "float32"),
+}
+SEMAPHORES = ["lu", "lv1", "lv2", "arr", "sent", "harr", "fin", "st"]
+
+LOW, HIGH, ALL = 0x00FF, 0xFF00, 0xFFFF
+CHIP_BASE = 48
+
+
+def _dst(topo, d, core):
+    rid, pid = topo.addr(d, core)
+    return DstId(rid=rid, pnc=pid)
+
+
+def rank_program(g, core, T, topo):
+    S = topo.host(core)
+    helper = lambda h: 128 * (h % 4) + CHIP_BASE
+    sem = T.sem
+
+    if core == helper(S):
+        g.wait_ge(sem.harr, 32)
+        ranks = [128 * S + CHIP_BASE + 2, 128 * S + CHIP_BASE + 3]
+        g.remote_dma_fused([RemoteDMATransfer(
+            dst_ids=[_dst(topo, r, core) for r in ranks], dma_engine_mask=ALL, remote_sem=sem.fin,
+            srcs=[T.xh[k] for k in range(4)], dsts=[T.fin[:], T.fin[:]], alu_op=1)], local_sem=sem.sent)
+        g.wait_ge(sem.sent, 16)
+        return
+
+    rank = T.rank_of(core)
+    if rank is None:
+        return
+    side = rank % 2
+    d = 1 if side == 0 else -1
+    nxt, prv, dg = (S + d) % 4, (S - d) % 4, (S + 2) % 4
+    peer = core + 1 if side == 0 else core - 1
+    fwd = 128 * nxt + core % 128
+
+    hb = lambda k: T.x[:, 128 * k:128 * k + 128]
+    g.sync.dma_start(T.xh[dg], hb(dg)).then_inc(sem.lu, 16)
+    g.scalar.dma_start(T.xh[prv], hb(prv)).then_inc(sem.lu, 16)
+    g.sync.dma_start(T.xh[nxt], hb(nxt)).then_inc(sem.lv1, 16)
+    g.scalar.dma_start(T.xh[S], hb(S)).then_inc(sem.lv2, 16)
+
+    g.wait_ge(sem.lu, 32)
+    g.remote_dma_fused([
+        RemoteDMATransfer(dst_ids=[_dst(topo, fwd, core)], dma_engine_mask=LOW, remote_sem=sem.arr,
+                          src=T.xh[dg], dst=T.ld[:], alu_op=0),
+        RemoteDMATransfer(dst_ids=[_dst(topo, peer, core)], dma_engine_mask=HIGH, remote_sem=sem.arr,
+                          src=T.xh[prv], dst=T.lp[:], alu_op=0),
+    ], local_sem=sem.sent)
+
+    g.wait_ge(sem.lv2, 16)
+    rid, pid = topo.addr(helper(S), core)
+    g.remote_dma(T.xh[side], T.xh[S], sem.harr, sem.sent, pid, rid, HIGH)
+
+    g.wait_ge(sem.arr, 16)
+    g.wait_ge(sem.lv1, 16)
+    g.remote_dma_fused([RemoteDMATransfer(
+        dst_ids=[_dst(topo, helper(nxt), core)], dma_engine_mask=LOW, remote_sem=sem.harr,
+        srcs=[T.xh[nxt], T.lp[:], T.ld[:]], dsts=[T.xh[2 + side]], alu_op=1)], local_sem=sem.sent)
+
+    g.sync.wait_ge(sem.fin, 16)
+    g.sync.dma_start(T.y[:, :], T.fin[:, 64 * side:64 * side + 64]).then_inc(sem.st, 16)
+
+    g.wait_ge(sem.sent, 32)
+    g.wait_ge(sem.st, 16)

@@ -1,15 +1,16 @@
 from concourse.bass import DstId, RemoteDMATransfer
 
 SCRATCH = {
-    "xh": ("dram", [4, 128, 128], "float32"),
-    "lp": ("dram", [128, 128], "float32"),
-    "ld": ("dram", [128, 128], "float32"),
-    "fin": ("dram", [128, 128], "float32"),
+    "xh": ("dram", [4, 2, 128, 64], "float32"),
+    "lp": ("dram", [2, 128, 64], "float32"),
+    "ld": ("dram", [2, 128, 64], "float32"),
+    "fin": ("dram", [2, 128, 64], "float32"),
 }
-SEMAPHORES = ["lu", "lv1", "lv2", "arr", "sent", "harr", "fin", "st"]
+SEMAPHORES = ["lu", "lv", "arr", "sent", "harr", "fin", "st"]
 
-LOW, HIGH, ALL = 0x00FF, 0xFF00, 0xFFFF
 CHIP_BASE = 48
+OFF = (0x000F, 0x00F0)
+ON = (0x0F00, 0xF000)
 
 
 def _dst(topo, d, core):
@@ -19,15 +20,16 @@ def _dst(topo, d, core):
 
 def rank_program(g, core, T, topo):
     S = topo.host(core)
-    helper = lambda h: 128 * (h % 4) + CHIP_BASE
+    helper = lambda host, lane: 128 * (host % 4) + CHIP_BASE + lane
     sem = T.sem
 
-    if core == helper(S):
-        g.wait_ge(sem.harr, 32)
+    if core in (helper(S, 0), helper(S, 1)):
+        lane = core - helper(S, 0)
+        g.wait_ge(sem.harr, 16)
         ranks = [128 * S + CHIP_BASE + 2, 128 * S + CHIP_BASE + 3]
         g.remote_dma_fused([RemoteDMATransfer(
-            dst_ids=[_dst(topo, r, core) for r in ranks], dma_engine_mask=ALL, remote_sem=sem.fin,
-            srcs=[T.xh[k] for k in range(4)], dsts=[T.fin[:], T.fin[:]], alu_op=1)], local_sem=sem.sent)
+            dst_ids=[_dst(topo, r, core) for r in ranks], dma_engine_mask=0xFFFF, remote_sem=sem.fin,
+            srcs=[T.xh[k, 0] for k in range(4)], dsts=[T.fin[lane], T.fin[lane]], alu_op=1)], local_sem=sem.sent)
         g.wait_ge(sem.sent, 16)
         return
 
@@ -43,29 +45,28 @@ def rank_program(g, core, T, topo):
     hb = lambda k: T.x[:, 128 * k:128 * k + 128]
     g.sync.dma_start(T.xh[dg], hb(dg)).then_inc(sem.lu, 16)
     g.scalar.dma_start(T.xh[prv], hb(prv)).then_inc(sem.lu, 16)
-    g.sync.dma_start(T.xh[nxt], hb(nxt)).then_inc(sem.lv1, 16)
-    g.scalar.dma_start(T.xh[S], hb(S)).then_inc(sem.lv2, 16)
+    g.sync.dma_start(T.xh[nxt], hb(nxt)).then_inc(sem.lv, 16)
+    g.scalar.dma_start(T.xh[S], hb(S)).then_inc(sem.lv, 16)
 
     g.wait_ge(sem.lu, 32)
-    g.remote_dma_fused([
-        RemoteDMATransfer(dst_ids=[_dst(topo, fwd, core)], dma_engine_mask=LOW, remote_sem=sem.arr,
-                          src=T.xh[dg], dst=T.ld[:], alu_op=0),
-        RemoteDMATransfer(dst_ids=[_dst(topo, peer, core)], dma_engine_mask=HIGH, remote_sem=sem.arr,
-                          src=T.xh[prv], dst=T.lp[:], alu_op=0),
-    ], local_sem=sem.sent)
+    g.remote_dma_fused(
+        [RemoteDMATransfer(dst_ids=[_dst(topo, fwd, core)], dma_engine_mask=OFF[h], remote_sem=sem.arr,
+                           src=T.xh[dg, h], dst=T.ld[h], alu_op=0) for h in range(2)] +
+        [RemoteDMATransfer(dst_ids=[_dst(topo, peer, core)], dma_engine_mask=ON[h], remote_sem=sem.arr,
+                           src=T.xh[prv, h], dst=T.lp[h], alu_op=0) for h in range(2)],
+        local_sem=sem.sent)
 
-    g.wait_ge(sem.lv2, 16)
-    rid, pid = topo.addr(helper(S), core)
-    g.remote_dma(T.xh[side], T.xh[S], sem.harr, sem.sent, pid, rid, HIGH)
-
+    g.wait_ge(sem.lv, 32)
     g.wait_ge(sem.arr, 16)
-    g.wait_ge(sem.lv1, 16)
-    g.remote_dma_fused([RemoteDMATransfer(
-        dst_ids=[_dst(topo, helper(nxt), core)], dma_engine_mask=LOW, remote_sem=sem.harr,
-        srcs=[T.xh[nxt], T.lp[:], T.ld[:]], dsts=[T.xh[2 + side]], alu_op=1)], local_sem=sem.sent)
+    g.remote_dma_fused(
+        [RemoteDMATransfer(dst_ids=[_dst(topo, helper(nxt, h), core)], dma_engine_mask=OFF[h], remote_sem=sem.harr,
+                           srcs=[T.xh[nxt, h], T.lp[h], T.ld[h]], dsts=[T.xh[2 + side, 0]], alu_op=1) for h in range(2)] +
+        [RemoteDMATransfer(dst_ids=[_dst(topo, helper(S, h), core)], dma_engine_mask=ON[h], remote_sem=sem.harr,
+                           srcs=[T.xh[S, h]], dsts=[T.xh[side, 0]], alu_op=0) for h in range(2)],
+        local_sem=sem.sent)
 
-    g.sync.wait_ge(sem.fin, 16)
-    g.sync.dma_start(T.y[:, :], T.fin[:, 64 * side:64 * side + 64]).then_inc(sem.st, 16)
+    g.sync.wait_ge(sem.fin, 32)
+    g.sync.dma_start(T.y[:, :], T.fin[:, side:128:2, :]).then_inc(sem.st, 16)
 
     g.wait_ge(sem.sent, 32)
     g.wait_ge(sem.st, 16)

from concourse.bass import DstId, RemoteDMATransfer

SCRATCH = {
    "xh": ("dram", [4, 2, 128, 64], "float32"),
    "lp": ("dram", [2, 128, 64], "float32"),
    "ld": ("dram", [2, 128, 64], "float32"),
    "fin": ("dram", [2, 128, 64], "float32"),
}
SEMAPHORES = ["lu", "lv", "arr", "sent", "harr", "fin", "st"]

CHIP_BASE = 48
OFF = (0x000F, 0x00F0)
ON = (0x0F00, 0xF000)


def _dst(topo, d, core):
    rid, pid = topo.addr(d, core)
    return DstId(rid=rid, pnc=pid)


def rank_program(g, core, T, topo):
    S = topo.host(core)
    helper = lambda host, lane: 128 * (host % 4) + CHIP_BASE + lane
    sem = T.sem

    if core in (helper(S, 0), helper(S, 1)):
        lane = core - helper(S, 0)
        g.wait_ge(sem.harr, 16)
        ranks = [128 * S + CHIP_BASE + 2, 128 * S + CHIP_BASE + 3]
        g.remote_dma_fused([RemoteDMATransfer(
            dst_ids=[_dst(topo, r, core) for r in ranks], dma_engine_mask=0xFFFF, remote_sem=sem.fin,
            srcs=[T.xh[k, 0] for k in range(4)], dsts=[T.fin[lane], T.fin[lane]], alu_op=1)], local_sem=sem.sent)
        g.wait_ge(sem.sent, 16)
        return

    rank = T.rank_of(core)
    if rank is None:
        return
    side = rank % 2
    d = 1 if side == 0 else -1
    nxt, prv, dg = (S + d) % 4, (S - d) % 4, (S + 2) % 4
    peer = core + 1 if side == 0 else core - 1
    fwd = 128 * nxt + core % 128

    hb = lambda k: T.x[:, 128 * k:128 * k + 128]
    g.sync.dma_start(T.xh[dg], hb(dg)).then_inc(sem.lu, 16)
    g.scalar.dma_start(T.xh[prv], hb(prv)).then_inc(sem.lu, 16)
    g.sync.dma_start(T.xh[nxt], hb(nxt)).then_inc(sem.lv, 16)
    g.scalar.dma_start(T.xh[S], hb(S)).then_inc(sem.lv, 16)

    g.wait_ge(sem.lu, 32)
    g.remote_dma_fused(
        [RemoteDMATransfer(dst_ids=[_dst(topo, fwd, core)], dma_engine_mask=OFF[h], remote_sem=sem.arr,
                           src=T.xh[dg, h], dst=T.ld[h], alu_op=0) for h in range(2)] +
        [RemoteDMATransfer(dst_ids=[_dst(topo, peer, core)], dma_engine_mask=ON[h], remote_sem=sem.arr,
                           src=T.xh[prv, h], dst=T.lp[h], alu_op=0) for h in range(2)],
        local_sem=sem.sent)

    g.wait_ge(sem.lv, 32)
    g.wait_ge(sem.arr, 16)
    g.remote_dma_fused(
        [RemoteDMATransfer(dst_ids=[_dst(topo, helper(nxt, h), core)], dma_engine_mask=OFF[h], remote_sem=sem.harr,
                           srcs=[T.xh[nxt, h], T.lp[h], T.ld[h]], dsts=[T.xh[2 + side, 0]], alu_op=1) for h in range(2)] +
        [RemoteDMATransfer(dst_ids=[_dst(topo, helper(S, h), core)], dma_engine_mask=ON[h], remote_sem=sem.harr,
                           srcs=[T.xh[S, h]], dsts=[T.xh[side, 0]], alu_op=0) for h in range(2)],
        local_sem=sem.sent)

    g.sync.wait_ge(sem.fin, 32)
    g.sync.dma_start(T.y[:, :], T.fin[:, side:128:2, :]).then_inc(sem.st, 16)

    g.wait_ge(sem.sent, 32)
    g.wait_ge(sem.st, 16)
